import numpy as np
import ml_dtypes


def mxq(x, axis, fmt="e4m3"):
    dtype, down = {"e4m3": (ml_dtypes.float8_e4m3fn, 7), "e5m2": (ml_dtypes.float8_e5m2, 14)}[fmt]
    v = np.moveaxis(np.asarray(x, np.float32).astype(ml_dtypes.bfloat16).astype(np.float64), axis, -1)
    blocks = v.reshape(v.shape[:-1] + (-1, 32))
    amax = np.abs(blocks).max(-1, keepdims=True)
    byte = np.maximum(np.where(amax > 0, np.frexp(amax)[1] - 1 + 127, 0) - down, 1)
    scale = np.exp2(byte - 127.0)
    codes = (blocks / scale).astype(np.float32).astype(dtype).astype(np.float64)
    return np.moveaxis((codes * scale).reshape(v.shape), -1, axis)


WIDE = False


def mx_kscale(k):
    if not WIDE:
        return np.ones(k)
    levels = np.array([10, -10, 5, -5, 0])
    if k % 512:
        return np.exp2(np.random.permutation(np.resize(levels, k // 32))).repeat(32)
    a = np.empty((k // 512, 16))
    for p in range(k // 512):
        a[p, :8] = np.random.permutation(np.resize(levels, 8))
        for g in range(8):
            far = levels[np.abs(levels - a[p, g]) >= 10]
            a[p, g + 8] = far[np.random.randint(len(far))]
    return np.exp2(a.ravel()).repeat(32)


def f64(x):
    return np.asarray(x).astype(np.float64)


def striped(idx):
    return np.tile(idx.reshape(-1, 16).T, (8, 1)).astype(np.uint16)


def unstriped(offs):
    return offs[:16].T.reshape(-1).astype(np.int64)


def striped8(idx):
    return np.concatenate([x.reshape(-1, 16).T for x in idx]).astype(np.uint16)


def runs(offs, k):
    lists = np.stack([offs[16 * r : 16 * r + 16].T.reshape(-1) for r in range(8)]).astype(np.int64)
    return lists[np.arange(k) % 512 // 64]


def pack_weight(w):
    k, n = w.shape
    w = f64(np.asarray(w, np.float32).astype(ml_dtypes.bfloat16)).reshape(k // 32, 32, n)
    amax = np.abs(w).max(1)
    byte = np.clip(np.where(amax > 0, np.frexp(amax)[1] - 1 + 127 - 7, 1), 1, 254)
    scaled = (w * np.exp2(127.0 - byte)[:, None, :]).reshape(k, n).astype(np.float32)
    words = np.ascontiguousarray(scaled.reshape(k // 512, 128, 4, n).transpose(0, 1, 3, 2)).astype(ml_dtypes.float8_e4m3fn).view(np.uint8)
    return words, np.ascontiguousarray(byte.astype(np.uint8).reshape(k // 512, 16, n))


def unpack_weight(words, scales):
    g, p, n, _ = words.shape
    vals = np.ascontiguousarray(words).view(ml_dtypes.float8_e4m3fn).astype(np.float64) * np.repeat(np.exp2(scales.astype(np.float64) - 127.0), 8, axis=1)[..., None]
    return vals.transpose(0, 1, 3, 2).reshape(g * 512, n)


def sigmoid(v):
    return 1.0 / (1.0 + np.exp(-np.maximum(v, -700.0)))


K, T, S, N, G, H, W = 512, 2048, 512, 512, 2048, 512, 256


def setup_inputs():
    n = np.random.standard_normal
    s = mx_kscale(K)[:, None]
    u = mx_kscale(S)
    packed_xT = pack_weight(n((K, T)) * s)
    packed_dT = pack_weight(n((K, G)) / s)
    perm = np.random.permutation(S)
    return {
        "x_words": packed_xT[0],
        "x_scales": packed_xT[1],
        "d_words": packed_dT[0],
        "d_scales": packed_dT[1],
        "sl": np.random.uniform(1.5, 3.0, (H, 1)).astype(np.float32),
        "th": (0.5 * n((H, 1))).astype(np.float32),
        "gn": (np.random.uniform(0.5, 1.5, (H, 1)) * u[:, None]).astype(np.float32),
        "w1": (n((H, N)) / np.sqrt(H) / u[:, None]).astype(np.float32),
        "offs": striped(np.random.permutation(T)[:S]),
        "k1": striped8(np.random.randint(0, G, (8, H))),
        "n1": striped8(np.stack([np.random.permutation(S) for _ in range(8)])),
        "n2": striped8(np.stack([np.random.permutation(S) for _ in range(8)])),
        "n3": striped(perm[:W]),
        "n4": striped(perm[W:]),
    }


def reference(x_words, x_scales, d_words, d_scales, sl, th, gn, w1, offs, k1, n1, n2, n3, n4):
    d_k1 = unpack_weight(d_words, d_scales)[np.arange(K)[:, None], runs(k1, K)]
    xq = unpack_weight(x_words, x_scales)[:, unstriped(offs)]
    h = 0.0625 * (d_k1.T @ xq)
    sg = sigmoid(f64(sl) * (h[np.arange(H)[:, None], runs(n1, H)] - f64(th)))
    z = f64(gn) * (1.5 * (h * (sg - (sg[np.arange(H)[:, None], runs(n2, H)]))))
    h2 = mxq(f64(w1), 0, "e4m3").T @ mxq(z, 0, "e4m3")
    pa = h2[:, unstriped(n3)]
    pb = h2[:, unstriped(n4)]
    rb = np.maximum(0.5 * pa, pb)
    ra = pb - pa
    ds = np.zeros((N, S))
    ds[:, unstriped(n3)] = ra
    out = ds.copy()
    out[:, unstriped(n4)] = rb
    return out

@@ -1,0 +1,210 @@
+from contextlib import ExitStack
+
+import concourse.mybir as mybir
+
+F32 = mybir.dt.float32
+BF16 = mybir.dt.bfloat16
+I32 = mybir.dt.int32
+U32 = mybir.dt.uint32
+U16 = mybir.dt.uint16
+U8 = mybir.dt.uint8
+FP8X4 = mybir.dt.float8_e4m3fn_x4
+ALU = mybir.AluOpType
+ACT = mybir.ActivationFunctionType
+
+P = 128
+PACK = 4
+T = 2048
+S = 512
+W = 256
+FLOPS = 2 * 2 * 512 * 512 * 512
+
+
+def tile_picked_pqlayedblift_none_p_kernel(tc, x_words, x_scales, d_words, d_scales, sl, th, gn, w1, offs, k1, n1, n2, n3, n4, out):
+    nc = tc.nc
+    with ExitStack() as ctx:
+        sb = ctx.enter_context(tc.tile_pool(name="sb", bufs=1))
+        ps = ctx.enter_context(tc.psum_pool(name="ps", bufs=1))
+
+        def tile(name, shape, dtype, tag=None):
+            return sb.tile(shape, dtype, name=name, tag=tag or name, align_bytes=64)
+
+        def load_list(name, src):
+            t = tile(name, list(src.shape), U16)
+            nc.sync.dma_start(t[:], src)
+            return t
+
+        def load_rows(name, src):
+            t = tile(name, [P, PACK], F32)
+            nc.sync.dma_start(t[:], src.rearrange("(p t) o -> p (t o)", t=PACK))
+            return t
+
+        def clock(name, ap, dtype):
+            c = tile(name, [P, 1], dtype)
+            nc.gpsimd.tensor_copy(c[:], ap)
+
+        halves = [slice(W * a, W * (a + 1)) for a in range(2)]
+        whole = slice(0, S)
+
+        def entries(cols):
+            return slice(cols.start // 16, cols.stop // 16)
+
+        d_byte_table = tile("d_byte_table", [P, T], U8)
+        x_byte_table = tile("x_byte_table", [P, T], U8)
+        nc.vector.memset(d_byte_table[:].bitcast(I32), 0)
+        nc.gpsimd.memset(x_byte_table[:].bitcast(I32), 0)
+
+        k1_t = load_list("k1_t", k1)
+        offs_t = load_list("offs_t", offs)
+        n1_t = load_list("n1_t", n1)
+        n2_t = load_list("n2_t", n2)
+        n3_t = load_list("n3_t", n3)
+        n4_t = load_list("n4_t", n4)
+        nc.gpsimd.dma_start(d_byte_table[0:P:8, :].bitcast(I32), d_scales[0].bitcast(I32))
+        for q in range(4):
+            nc.gpsimd.dma_start(x_byte_table[32 * q : 32 * q + 4, :].bitcast(I32), x_scales[0, 4 * q : 4 * q + 4, :].bitcast(I32))
+        d_word_table = tile("d_word_table", [P, T], U32)
+        nc.sync.dma_start(d_word_table[:].bitcast(I32), d_words[0].rearrange("p n t -> p (n t)").bitcast(I32))
+        x_word_table = tile("x_word_table", [P, T], U32)
+        nc.sync.dma_start(x_word_table[:].bitcast(I32), x_words[0].rearrange("p n t -> p (n t)").bitcast(I32))
+        sl_t = load_rows("sl_t", sl)
+        th_t = load_rows("th_t", th)
+        gn_t = load_rows("gn_t", gn)
+        w_raw = tile("w_raw", [P, PACK, S], F32)
+        nc.sync.dma_start(w_raw[:], w1.rearrange("(p t) m -> p t m", t=PACK))
+
+        d_bytes = tile("d_bytes", [P, S], U8)
+        nc.vector.tensor_copy(d_bytes[:], d_byte_table[:].indirect(k1_t[:]))
+        d_bytes_dealt = tile("d_bytes_dealt", [P, S], U8)
+        nc.vector.tensor_copy(d_bytes_dealt[:].rearrange("p (t m) -> p t m", t=PACK), d_bytes[:].rearrange("p (m t) -> p t m", t=PACK))
+        d_plane = tile("d_plane", [P, S], U8)
+        nc.vector.tensor_copy(d_plane[:].bitcast(I32), d_bytes_dealt[:].bitcast(I32))
+        for r in range(1, 4):
+            nc.scalar.dma_start(d_plane[r:P:32, :].bitcast(I32), d_bytes_dealt[8 * r : P : 32, :].bitcast(I32))
+        d_codes = tile("d_codes", [P, S], U32)
+        d_codes_dealt = tile("d_codes_dealt", [P, S], U32)
+        nc.vector.tensor_copy(d_codes[:], d_word_table[:].indirect(k1_t[:]))
+        nc.vector.tensor_copy(d_codes_dealt[:].rearrange("p (t m) -> p t m", t=PACK), d_codes[:].rearrange("p (m t) -> p t m", t=PACK))
+        x_plane = tile("x_plane", [P, S], U8, tag="d_codes")
+        nc.vector.tensor_copy(x_plane[:], x_byte_table[:].indirect(offs_t[:]))
+        x_codes = tile("x_codes", [P, S], U32)
+        for cols in halves:
+            nc.vector.tensor_copy(x_codes[:, cols], x_word_table[:].indirect(offs_t[:, entries(cols)]))
+        bias_t = tile("bias_t", [P, PACK], F32)
+        nc.vector.scalar_tensor_tensor(bias_t[:], sl_t[:], -1.0, th_t[:], ALU.mult, ALU.mult)
+        gain_t = tile("gain_t", [P, PACK], F32)
+        nc.vector.tensor_scalar(gain_t[:], gn_t[:], -1.5 * 0.0625, None, ALU.mult)
+
+        def product(bank, codes_l, plane_l, block, codes_r, plane_r, cols):
+            acc = ps.tile([P, cols.stop - cols.start], F32, name=f"acc_{bank}", tag=f"bank{bank}")
+            rows = slice(P * block, P * (block + 1))
+            nc.tensor.matmul_mx(out=acc[:], lhsT=codes_l[:, rows].bitcast(FP8X4), lhsT_scale=plane_l[:, rows],
+                                rhs=codes_r[:, cols].bitcast(FP8X4), rhs_scale=plane_r[:, cols], start=True, stop=True)
+            return acc
+
+        pieces = [(0, halves[0]), (0, halves[1]), (1, whole), (2, whole), (3, whole)]
+        h_acc = [[] for t in range(PACK)]
+        for bank, (t, cols) in enumerate(pieces):
+            h_acc[t].append((cols, product(bank, d_codes_dealt, d_plane, t, x_codes, x_plane, cols)))
+
+        sg = []
+        for t in range(PACK):
+            h_t = tile(f"h{t}", [P, S], F32, tag="h")
+            for cols, acc in h_acc[t]:
+                if t == 0:
+                    nc.vector.tensor_scalar(h_t[:, cols], acc[:], 0.0625, None, ALU.mult)
+                else:
+                    nc.scalar.activation(h_t[:, cols], acc[:], ACT.Copy, scale=0.0625)
+            sg_t = tile(f"sg{t}", [P, S], F32)
+            for cols in halves:
+                nc.scalar.activation(sg_t[:, cols], h_t[:].indirect(n1_t[:, entries(cols)]), ACT.Sigmoid,
+                                     bias=bias_t[:, t : t + 1], scale=sl_t[:, t : t + 1])
+            sg.append(sg_t)
+
+        w_codes = tile("w_codes", [P, S], U32)
+        w_plane = tile("w_plane", [P, S], U8)
+
+        def round_w(copy, name, tag, cols):
+            grouped = tile(name, [P, W, PACK], BF16, tag=tag)
+            copy(grouped[:].rearrange("p (c i) t -> p c t i", i=4), w_raw[:, :, cols].rearrange("p t (c i) -> p c t i", i=4))
+            return grouped
+
+        def quantize(codes, plane, cols, grouped):
+            nc.vector.quantize_mx(out=codes[:, cols].bitcast(FP8X4), scales=plane[:, cols], in_=grouped.rearrange("p c t -> p (c t)"))
+
+        quantize(w_codes, w_plane, halves[0], round_w(nc.vector.tensor_copy, "w_grouped0", "sg_copy0", halves[0])[:])
+
+        z_planes = tile("z_planes", [P, PACK, S], BF16)
+        last = PACK - 1
+        for t in range(last):
+            sg_copy = tile(f"sg_copy{t}", [P, S], F32)
+            nc.vector.tensor_copy(sg_copy[:], sg[t][:])
+            diff = tile(f"diff{t}", [P, S], F32)
+            for cols in halves:
+                nc.vector.tensor_tensor(diff[:, cols], sg[t][:].indirect(n2_t[:, entries(cols)]), sg_copy[:, cols], ALU.subtract)
+            for cols, acc in h_acc[t]:
+                nc.vector.scalar_tensor_tensor(z_planes[:, t, cols], diff[:, cols], gain_t[:, t : t + 1], acc[:], ALU.mult, ALU.mult)
+
+        fetched = tile("fetched", [P, S], F32)
+        diff = tile("diff_last", [P, S], F32)
+        z_grouped = tile("z_grouped", [P, S, PACK], BF16)
+        z_codes = tile("z_codes", [P, S], U32)
+        z_plane = tile("z_plane", [P, S], U8)
+        acc = h_acc[last][0][1]
+        for cols in halves:
+            nc.scalar.activation(fetched[:, cols], sg[last][:].indirect(n2_t[:, entries(cols)]), ACT.Copy)
+        w_grouped = round_w(nc.scalar.copy, "w_grouped1", "h", halves[1])
+        for cols in halves:
+            nc.vector.tensor_tensor(diff[:, cols], fetched[:, cols], sg[last][:, cols], ALU.subtract)
+        for cols in halves:
+            nc.vector.scalar_tensor_tensor(z_planes[:, last, cols], diff[:, cols], gain_t[:, last : last + 1], acc[:, cols], ALU.mult, ALU.mult)
+        SPLIT = 96
+        for eng, cols in [(nc.scalar.copy, slice(0, SPLIT)), (nc.vector.tensor_copy, slice(SPLIT, W)), (nc.scalar.copy, slice(W, W + SPLIT)), (nc.vector.tensor_copy, slice(W + SPLIT, S))]:
+            eng(z_grouped[:, cols, :].rearrange("p (c i) t -> p c t i", i=4), z_planes[:, :, cols].rearrange("p t (c i) -> p c t i", i=4))
+        for cols in halves:
+            quantize(z_codes, z_plane, cols, z_grouped[:, cols, :])
+        quantize(w_codes, w_plane, halves[1], w_grouped[:])
+
+        pieces = [(0, halves[0]), (1, halves[0]), (0, halves[1]), (1, halves[1]), (2, whole), (3, whole)]
+        h2_acc = [[] for u in range(PACK)]
+        for n, (u, cols) in enumerate(pieces):
+            h2_acc[u].append((cols, product((5 + n) % 8, w_codes, w_plane, u, z_codes, z_plane, cols)))
+        h2 = [tile(f"h2_{u}", [P, S], F32) for u in range(PACK)]
+        pa = [tile(f"pa{u}", [P, W], F32) for u in range(PACK)]
+        ra = [tile(f"ra{u}", [P, W], F32) for u in range(PACK)]
+        rise = [tile(f"rise{u}", [P, W], F32) for u in range(PACK)]
+        res = [tile(f"res{u}", [P, S], F32, tag="h2_3" if u == 1 else None) for u in range(PACK)]
+
+        def pair(u):
+            nc.vector.tensor_tensor(ra[u][:], h2[u][:].indirect(n4_t[:]), pa[u][:], ALU.subtract)
+            nc.vector.scalar_tensor_tensor(rise[u][:], pa[u][:], -0.5, ra[u][:], ALU.mult, ALU.max)
+
+        def put_rb(u):
+            nc.vector.tensor_tensor(res[u][:].indirect(n4_t[:]), rise[u][:], pa[u][:], ALU.add)
+
+        def put_ra(u):
+            nc.scalar.activation(res[u][:].indirect(n3_t[:]), ra[u][:], ACT.Copy)
+
+        def store(u, eng):
+            eng.dma_start(out[P * u : P * (u + 1), :], res[u][:])
+
+        nc.scalar.copy(h2[0][:, halves[0]], h2_acc[0][0][1][:])
+        nc.vector.tensor_copy(h2[0][:, halves[1]], h2_acc[0][1][1][:])
+        nc.vector.tensor_copy(pa[0][:], h2[0][:].indirect(n3_t[:]))
+        for u in range(1, PACK):
+            for cols, acc in h2_acc[u]:
+                nc.scalar.copy(h2[u][:, cols], acc[:])
+            nc.scalar.activation(pa[u][:], h2[u][:].indirect(n3_t[:]), ACT.Copy)
+        pair(0)
+        put_rb(0)
+        for u in range(1, PACK):
+            pair(u)
+        put_ra(0)
+        store(0, nc.sync)
+        put_rb(1)
+        for u in range(2, PACK):
+            put_ra(u)
+            put_rb(u)
+            store(u, nc.sync)
+        put_ra(1)
+        store(1, nc.scalar)

@@ -56,22 +56,16 @@ def tile_picked_pqlayedblift_none_p_kernel(tc, x_words, x_scales, d_words, d_sca
 
         k1_t = load_list("k1_t", k1)
         offs_t = load_list("offs_t", offs)
-        n1_t = load_list("n1_t", n1)
-        n2_t = load_list("n2_t", n2)
-        n3_t = load_list("n3_t", n3)
-        n4_t = load_list("n4_t", n4)
-        nc.gpsimd.dma_start(d_byte_table[0:P:8, :].bitcast(I32), d_scales[0].bitcast(I32))
+        nc.sync.dma_start(d_byte_table[0:P:8, :].bitcast(I32), d_scales[0].bitcast(I32))
         for q in range(4):
-            nc.gpsimd.dma_start(x_byte_table[32 * q : 32 * q + 4, :].bitcast(I32), x_scales[0, 4 * q : 4 * q + 4, :].bitcast(I32))
+            nc.sync.dma_start(x_byte_table[32 * q : 32 * q + 4, :].bitcast(I32), x_scales[0, 4 * q : 4 * q + 4, :].bitcast(I32))
         d_word_table = tile("d_word_table", [P, T], U32)
         nc.sync.dma_start(d_word_table[:].bitcast(I32), d_words[0].rearrange("p n t -> p (n t)").bitcast(I32))
         x_word_table = tile("x_word_table", [P, T], U32)
         nc.sync.dma_start(x_word_table[:].bitcast(I32), x_words[0].rearrange("p n t -> p (n t)").bitcast(I32))
+        n1_t = load_list("n1_t", n1)
         sl_t = load_rows("sl_t", sl)
         th_t = load_rows("th_t", th)
-        gn_t = load_rows("gn_t", gn)
-        w_raw = tile("w_raw", [P, PACK, S], F32)
-        nc.sync.dma_start(w_raw[:], w1.rearrange("(p t) m -> p t m", t=PACK))
 
         d_bytes = tile("d_bytes", [P, S], U8)
         nc.vector.tensor_copy(d_bytes[:], d_byte_table[:].indirect(k1_t[:]))
@@ -81,40 +75,47 @@ def tile_picked_pqlayedblift_none_p_kernel(tc, x_words, x_scales, d_words, d_sca
         nc.vector.tensor_copy(d_plane[:].bitcast(I32), d_bytes_dealt[:].bitcast(I32))
         for r in range(1, 4):
             nc.scalar.dma_start(d_plane[r:P:32, :].bitcast(I32), d_bytes_dealt[8 * r : P : 32, :].bitcast(I32))
+        x_plane = tile("x_plane", [P, S], U8)
+        nc.vector.tensor_copy(x_plane[:], x_byte_table[:].indirect(offs_t[:]))
+        w_raw = tile("w_raw", [P, PACK, S], F32, tag="x_byte_table")
+        nc.sync.dma_start(w_raw[:], w1.rearrange("(p t) m -> p t m", t=PACK))
+        n2_t = load_list("n2_t", n2)
+        gn_t = load_rows("gn_t", gn)
+        n3_t = load_list("n3_t", n3)
+        n4_t = load_list("n4_t", n4)
         d_codes = tile("d_codes", [P, S], U32)
         d_codes_dealt = tile("d_codes_dealt", [P, S], U32)
         nc.vector.tensor_copy(d_codes[:], d_word_table[:].indirect(k1_t[:]))
         nc.vector.tensor_copy(d_codes_dealt[:].rearrange("p (t m) -> p t m", t=PACK), d_codes[:].rearrange("p (m t) -> p t m", t=PACK))
-        x_plane = tile("x_plane", [P, S], U8, tag="d_codes")
-        nc.vector.tensor_copy(x_plane[:], x_byte_table[:].indirect(offs_t[:]))
         x_codes = tile("x_codes", [P, S], U32)
         for cols in halves:
             nc.vector.tensor_copy(x_codes[:, cols], x_word_table[:].indirect(offs_t[:, entries(cols)]))
         bias_t = tile("bias_t", [P, PACK], F32)
         nc.vector.scalar_tensor_tensor(bias_t[:], sl_t[:], -1.0, th_t[:], ALU.mult, ALU.mult)
         gain_t = tile("gain_t", [P, PACK], F32)
-        nc.vector.tensor_scalar(gain_t[:], gn_t[:], -1.5 * 0.0625, None, ALU.mult)
+        nc.vector.tensor_scalar(gain_t[:], gn_t[:], -1.5, None, ALU.mult)
 
-        def product(bank, codes_l, plane_l, block, codes_r, plane_r, cols):
-            acc = ps.tile([P, cols.stop - cols.start], F32, name=f"acc_{bank}", tag=f"bank{bank}")
+        def bank(name, shape, tag=None):
+            return ps.tile(shape, F32, name=name, tag=tag or name)
+
+        def product(acc, codes_l, plane_l, block, codes_r, plane_r, cols):
             rows = slice(P * block, P * (block + 1))
-            nc.tensor.matmul_mx(out=acc[:], lhsT=codes_l[:, rows].bitcast(FP8X4), lhsT_scale=plane_l[:, rows],
+            nc.tensor.matmul_mx(out=acc, lhsT=codes_l[:, rows].bitcast(FP8X4), lhsT_scale=plane_l[:, rows],
                                 rhs=codes_r[:, cols].bitcast(FP8X4), rhs_scale=plane_r[:, cols], start=True, stop=True)
             return acc
 
-        pieces = [(0, halves[0]), (0, halves[1]), (1, whole), (2, whole), (3, whole)]
-        h_acc = [[] for t in range(PACK)]
-        for bank, (t, cols) in enumerate(pieces):
-            h_acc[t].append((cols, product(bank, d_codes_dealt, d_plane, t, x_codes, x_plane, cols)))
-
-        sg = []
+        h, sg = [], []
         for t in range(PACK):
-            h_t = tile(f"h{t}", [P, S], F32, tag="h")
-            for cols, acc in h_acc[t]:
-                if t == 0:
-                    nc.vector.tensor_scalar(h_t[:, cols], acc[:], 0.0625, None, ALU.mult)
-                else:
-                    nc.scalar.activation(h_t[:, cols], acc[:], ACT.Copy, scale=0.0625)
+            h_t = tile(f"h{t}", [P, S], F32)
+            if t == 0:
+                for a, cols in enumerate(halves):
+                    acc = product(bank(f"h_first{a}", [P, W])[:], d_codes_dealt, d_plane, t, x_codes, x_plane, cols)
+                    nc.vector.tensor_scalar(h_t[:, cols], acc, 0.0625, None, ALU.mult)
+                h_rest = bank("h_rest", [P, PACK - 1, S], tag="h_first1")
+            else:
+                acc = product(h_rest[:, t - 1, :], d_codes_dealt, d_plane, t, x_codes, x_plane, whole)
+                nc.scalar.activation(h_t[:], acc, ACT.Copy, scale=0.0625)
+            h.append(h_t)
             sg_t = tile(f"sg{t}", [P, S], F32)
             for cols in halves:
                 nc.scalar.activation(sg_t[:, cols], h_t[:].indirect(n1_t[:, entries(cols)]), ACT.Sigmoid,
@@ -142,22 +143,20 @@ def tile_picked_pqlayedblift_none_p_kernel(tc, x_words, x_scales, d_words, d_sca
             diff = tile(f"diff{t}", [P, S], F32)
             for cols in halves:
                 nc.vector.tensor_tensor(diff[:, cols], sg[t][:].indirect(n2_t[:, entries(cols)]), sg_copy[:, cols], ALU.subtract)
-            for cols, acc in h_acc[t]:
-                nc.vector.scalar_tensor_tensor(z_planes[:, t, cols], diff[:, cols], gain_t[:, t : t + 1], acc[:], ALU.mult, ALU.mult)
+            nc.vector.scalar_tensor_tensor(z_planes[:, t, :], diff[:], gain_t[:, t : t + 1], h[t][:], ALU.mult, ALU.mult)
 
         fetched = tile("fetched", [P, S], F32)
         diff = tile("diff_last", [P, S], F32)
         z_grouped = tile("z_grouped", [P, S, PACK], BF16)
         z_codes = tile("z_codes", [P, S], U32)
         z_plane = tile("z_plane", [P, S], U8)
-        acc = h_acc[last][0][1]
         for cols in halves:
             nc.scalar.activation(fetched[:, cols], sg[last][:].indirect(n2_t[:, entries(cols)]), ACT.Copy)
-        w_grouped = round_w(nc.scalar.copy, "w_grouped1", "h", halves[1])
+        w_grouped = round_w(nc.scalar.copy, "w_grouped1", "h2", halves[1])
         for cols in halves:
             nc.vector.tensor_tensor(diff[:, cols], fetched[:, cols], sg[last][:, cols], ALU.subtract)
         for cols in halves:
-            nc.vector.scalar_tensor_tensor(z_planes[:, last, cols], diff[:, cols], gain_t[:, last : last + 1], acc[:, cols], ALU.mult, ALU.mult)
+            nc.vector.scalar_tensor_tensor(z_planes[:, last, cols], diff[:, cols], gain_t[:, last : last + 1], h[last][:, cols], ALU.mult, ALU.mult)
         SPLIT = 96
         for eng, cols in [(nc.scalar.copy, slice(0, SPLIT)), (nc.vector.tensor_copy, slice(SPLIT, W)), (nc.scalar.copy, slice(W, W + SPLIT)), (nc.vector.tensor_copy, slice(W + SPLIT, S))]:
             eng(z_grouped[:, cols, :].rearrange("p (c i) t -> p c t i", i=4), z_planes[:, :, cols].rearrange("p t (c i) -> p c t i", i=4))
@@ -168,7 +167,7 @@ def tile_picked_pqlayedblift_none_p_kernel(tc, x_words, x_scales, d_words, d_sca
         pieces = [(0, halves[0]), (1, halves[0]), (0, halves[1]), (1, halves[1]), (2, whole), (3, whole)]
         h2_acc = [[] for u in range(PACK)]
         for n, (u, cols) in enumerate(pieces):
-            h2_acc[u].append((cols, product((5 + n) % 8, w_codes, w_plane, u, z_codes, z_plane, cols)))
+            h2_acc[u].append((cols, product(bank(f"h2_acc{n}", [P, cols.stop - cols.start], tag=f"h_first{n - 4}" if n >= 4 else None)[:], w_codes, w_plane, u, z_codes, z_plane, cols)))
         h2 = [tile(f"h2_{u}", [P, S], F32) for u in range(PACK)]
         pa = [tile(f"pa{u}", [P, W], F32) for u in range(PACK)]
         ra = [tile(f"ra{u}", [P, W], F32) for u in range(PACK)]
@@ -188,12 +187,12 @@ def tile_picked_pqlayedblift_none_p_kernel(tc, x_words, x_scales, d_words, d_sca
         def store(u, eng):
             eng.dma_start(out[P * u : P * (u + 1), :], res[u][:])
 
-        nc.scalar.copy(h2[0][:, halves[0]], h2_acc[0][0][1][:])
-        nc.vector.tensor_copy(h2[0][:, halves[1]], h2_acc[0][1][1][:])
+        nc.scalar.copy(h2[0][:, halves[0]], h2_acc[0][0][1])
+        nc.vector.tensor_copy(h2[0][:, halves[1]], h2_acc[0][1][1])
         nc.vector.tensor_copy(pa[0][:], h2[0][:].indirect(n3_t[:]))
         for u in range(1, PACK):
             for cols, acc in h2_acc[u]:
-                nc.scalar.copy(h2[u][:, cols], acc[:])
+                nc.scalar.copy(h2[u][:, cols], acc)
             nc.scalar.activation(pa[u][:], h2[u][:].indirect(n3_t[:]), ACT.Copy)
         pair(0)
         put_rb(0)

@@ -61,16 +61,16 @@ def tile_picked_pqlayedblift_none_p_kernel(tc, x_words, x_scales, d_words, d_sca
             nc.sync.dma_start(x_byte_table[32 * q : 32 * q + 4, :].bitcast(I32), x_scales[0, 4 * q : 4 * q + 4, :].bitcast(I32))
         d_word_table = tile("d_word_table", [P, T], U32)
         nc.sync.dma_start(d_word_table[:].bitcast(I32), d_words[0].rearrange("p n t -> p (n t)").bitcast(I32))
-        x_word_table = tile("x_word_table", [P, T], U32)
-        nc.sync.dma_start(x_word_table[:].bitcast(I32), x_words[0].rearrange("p n t -> p (n t)").bitcast(I32))
         n1_t = load_list("n1_t", n1)
         sl_t = load_rows("sl_t", sl)
         th_t = load_rows("th_t", th)
+        x_word_table = tile("x_word_table", [P, T], U32)
+        nc.sync.dma_start(x_word_table[:].bitcast(I32), x_words[0].rearrange("p n t -> p (n t)").bitcast(I32))
 
         d_bytes = tile("d_bytes", [P, S], U8)
         nc.vector.tensor_copy(d_bytes[:], d_byte_table[:].indirect(k1_t[:]))
         d_bytes_dealt = tile("d_bytes_dealt", [P, S], U8)
-        nc.vector.tensor_copy(d_bytes_dealt[:].rearrange("p (t m) -> p t m", t=PACK), d_bytes[:].rearrange("p (m t) -> p t m", t=PACK))
+        nc.vector.tensor_copy(d_bytes_dealt[:].rearrange("p (t b i) -> p b t i", t=PACK, i=16), d_bytes[:].rearrange("p (b i t) -> p b t i", t=PACK, i=16))
         d_plane = tile("d_plane", [P, S], U8)
         nc.vector.tensor_copy(d_plane[:].bitcast(I32), d_bytes_dealt[:].bitcast(I32))
         for r in range(1, 4):
@@ -86,7 +86,7 @@ def tile_picked_pqlayedblift_none_p_kernel(tc, x_words, x_scales, d_words, d_sca
         d_codes = tile("d_codes", [P, S], U32)
         d_codes_dealt = tile("d_codes_dealt", [P, S], U32)
         nc.vector.tensor_copy(d_codes[:], d_word_table[:].indirect(k1_t[:]))
-        nc.vector.tensor_copy(d_codes_dealt[:].rearrange("p (t m) -> p t m", t=PACK), d_codes[:].rearrange("p (m t) -> p t m", t=PACK))
+        nc.vector.tensor_copy(d_codes_dealt[:].rearrange("p (t b i) -> p b t i", t=PACK, i=4), d_codes[:].rearrange("p (b i t) -> p b t i", t=PACK, i=4))
         x_codes = tile("x_codes", [P, S], U32)
         for cols in halves:
             nc.vector.tensor_copy(x_codes[:, cols], x_word_table[:].indirect(offs_t[:, entries(cols)]))
@@ -111,9 +111,8 @@ def tile_picked_pqlayedblift_none_p_kernel(tc, x_words, x_scales, d_words, d_sca
                 for a, cols in enumerate(halves):
                     acc = product(bank(f"h_first{a}", [P, W])[:], d_codes_dealt, d_plane, t, x_codes, x_plane, cols)
                     nc.vector.tensor_scalar(h_t[:, cols], acc, 0.0625, None, ALU.mult)
-                h_rest = bank("h_rest", [P, PACK - 1, S], tag="h_first1")
             else:
-                acc = product(h_rest[:, t - 1, :], d_codes_dealt, d_plane, t, x_codes, x_plane, whole)
+                acc = product(bank(f"h_acc{t}", [P, S], tag=f"h_first{t % 2}")[:], d_codes_dealt, d_plane, t, x_codes, x_plane, whole)
                 nc.scalar.activation(h_t[:], acc, ACT.Copy, scale=0.0625)
             h.append(h_t)
             sg_t = tile(f"sg{t}", [P, S], F32)
@@ -125,46 +124,58 @@ def tile_picked_pqlayedblift_none_p_kernel(tc, x_words, x_scales, d_words, d_sca
         w_codes = tile("w_codes", [P, S], U32)
         w_plane = tile("w_plane", [P, S], U8)
 
-        def round_w(copy, name, tag, cols):
-            grouped = tile(name, [P, W, PACK], BF16, tag=tag)
-            copy(grouped[:].rearrange("p (c i) t -> p c t i", i=4), w_raw[:, :, cols].rearrange("p t (c i) -> p c t i", i=4))
-            return grouped
-
         def quantize(codes, plane, cols, grouped):
             nc.vector.quantize_mx(out=codes[:, cols].bitcast(FP8X4), scales=plane[:, cols], in_=grouped.rearrange("p c t -> p (c t)"))
 
-        quantize(w_codes, w_plane, halves[0], round_w(nc.vector.tensor_copy, "w_grouped0", "sg_copy0", halves[0])[:])
+        def interleave(copy, grouped, planes):
+            copy(grouped.rearrange("p (c i) t -> p c t i", i=4), planes.rearrange("p t (c i) -> p c t i", i=4))
+
+        def quantize_w(a, tag):
+            w_grouped = tile(f"w_grouped{a}", [P, W, PACK], BF16, tag=tag)
+            interleave(nc.vector.tensor_copy, w_grouped[:], w_raw[:, :, halves[a]])
+            quantize(w_codes, w_plane, halves[a], w_grouped[:])
+
+        quantize_w(0, "sg_copy0")
 
         z_planes = tile("z_planes", [P, PACK, S], BF16)
-        last = PACK - 1
-        for t in range(last):
-            sg_copy = tile(f"sg_copy{t}", [P, S], F32)
-            nc.vector.tensor_copy(sg_copy[:], sg[t][:])
-            diff = tile(f"diff{t}", [P, S], F32)
-            for cols in halves:
-                nc.vector.tensor_tensor(diff[:, cols], sg[t][:].indirect(n2_t[:, entries(cols)]), sg_copy[:, cols], ALU.subtract)
-            nc.vector.scalar_tensor_tensor(z_planes[:, t, :], diff[:], gain_t[:, t : t + 1], h[t][:], ALU.mult, ALU.mult)
+        diff = [tile(f"diff{t}", [P, S], F32) for t in range(PACK)]
 
-        fetched = tile("fetched", [P, S], F32)
-        diff = tile("diff_last", [P, S], F32)
-        z_grouped = tile("z_grouped", [P, S, PACK], BF16)
+        def fetch_on_vector(t, parts):
+            span = slice(parts[0].start, parts[-1].stop)
+            sg_copy = tile(f"sg_copy{t}", [P, S], F32)
+            nc.vector.tensor_copy(sg_copy[:, span], sg[t][:, span])
+            for cols in parts:
+                nc.vector.tensor_tensor(diff[t][:, cols], sg[t][:].indirect(n2_t[:, entries(cols)]), sg_copy[:, cols], ALU.subtract)
+
+        def fetch_on_scalar(t, cols):
+            fetched = tile(f"fetched{t}_{cols.start}", [P, W], F32)
+            nc.scalar.activation(fetched[:], sg[t][:].indirect(n2_t[:, entries(cols)]), ACT.Copy)
+            nc.vector.tensor_tensor(diff[t][:, cols], fetched[:], sg[t][:, cols], ALU.subtract)
+
+        def make_z(t, cols):
+            nc.vector.scalar_tensor_tensor(z_planes[:, t, cols], diff[t][:, cols], gain_t[:, t : t + 1], h[t][:, cols], ALU.mult, ALU.mult)
+
+        for t in range(2):
+            fetch_on_vector(t, halves)
+            make_z(t, whole)
+        for cols in halves:
+            fetch_on_scalar(2, cols)
+        make_z(2, whole)
+        for cols in halves:
+            fetch_on_scalar(3, cols)
+        for cols in halves:
+            make_z(3, cols)
+
+        z_grouped = [tile(f"z_grouped{a}", [P, W, PACK], BF16) for a in range(2)]
         z_codes = tile("z_codes", [P, S], U32)
         z_plane = tile("z_plane", [P, S], U8)
-        for cols in halves:
-            nc.scalar.activation(fetched[:, cols], sg[last][:].indirect(n2_t[:, entries(cols)]), ACT.Copy)
-        w_grouped = round_w(nc.scalar.copy, "w_grouped1", "h2", halves[1])
-        for cols in halves:
-            nc.vector.tensor_tensor(diff[:, cols], fetched[:, cols], sg[last][:, cols], ALU.subtract)
-        for cols in halves:
-            nc.vector.scalar_tensor_tensor(z_planes[:, last, cols], diff[:, cols], gain_t[:, last : last + 1], h[last][:, cols], ALU.mult, ALU.mult)
-        SPLIT = 96
-        for eng, cols in [(nc.scalar.copy, slice(0, SPLIT)), (nc.vector.tensor_copy, slice(SPLIT, W)), (nc.scalar.copy, slice(W, W + SPLIT)), (nc.vector.tensor_copy, slice(W + SPLIT, S))]:
-            eng(z_grouped[:, cols, :].rearrange("p (c i) t -> p c t i", i=4), z_planes[:, :, cols].rearrange("p t (c i) -> p c t i", i=4))
-        for cols in halves:
-            quantize(z_codes, z_plane, cols, z_grouped[:, cols, :])
-        quantize(w_codes, w_plane, halves[1], w_grouped[:])
+        interleave(nc.scalar.copy, z_grouped[0][:], z_planes[:, :, halves[0]])
+        interleave(nc.vector.tensor_copy, z_grouped[1][:], z_planes[:, :, halves[1]])
+        for a in (1, 0):
+            quantize(z_codes, z_plane, halves[a], z_grouped[a][:])
+        quantize_w(1, "z_grouped0")
 
-        pieces = [(0, halves[0]), (1, halves[0]), (0, halves[1]), (1, halves[1]), (2, whole), (3, whole)]
+        pieces = [(0, halves[1]), (1, halves[1]), (0, halves[0]), (1, halves[0]), (2, whole), (3, whole)]
         h2_acc = [[] for u in range(PACK)]
         for n, (u, cols) in enumerate(pieces):
             h2_acc[u].append((cols, product(bank(f"h2_acc{n}", [P, cols.stop - cols.start], tag=f"h_first{n - 4}" if n >= 4 else None)[:], w_codes, w_plane, u, z_codes, z_plane, cols)))
@@ -187,8 +198,8 @@ def tile_picked_pqlayedblift_none_p_kernel(tc, x_words, x_scales, d_words, d_sca
         def store(u, eng):
             eng.dma_start(out[P * u : P * (u + 1), :], res[u][:])
 
-        nc.scalar.copy(h2[0][:, halves[0]], h2_acc[0][0][1])
-        nc.vector.tensor_copy(h2[0][:, halves[1]], h2_acc[0][1][1])
+        for cols, acc in h2_acc[0]:
+            nc.scalar.copy(h2[0][:, cols], acc)
         nc.vector.tensor_copy(pa[0][:], h2[0][:].indirect(n3_t[:]))
         for u in range(1, PACK):
             for cols, acc in h2_acc[u]:

@@ -77,12 +77,14 @@ def tile_picked_pqlayedblift_none_p_kernel(tc, x_words, x_scales, d_words, d_sca
             nc.scalar.dma_start(d_plane[r:P:32, :].bitcast(I32), d_bytes_dealt[8 * r : P : 32, :].bitcast(I32))
         x_plane = tile("x_plane", [P, S], U8)
         nc.vector.tensor_copy(x_plane[:], x_byte_table[:].indirect(offs_t[:]))
-        w_raw = tile("w_raw", [P, PACK, S], F32, tag="x_byte_table")
-        nc.sync.dma_start(w_raw[:], w1.rearrange("(p t) m -> p t m", t=PACK))
+        w_rows = w1.rearrange("(p t) m -> p t m", t=PACK)
+        w_raw = [tile("w_raw0", [P, PACK, W], F32, tag="x_byte_table"), tile("w_raw1", [P, PACK, W], F32)]
+        nc.sync.dma_start(w_raw[0][:], w_rows[:, :, halves[0]])
         n2_t = load_list("n2_t", n2)
         gn_t = load_rows("gn_t", gn)
         n3_t = load_list("n3_t", n3)
         n4_t = load_list("n4_t", n4)
+        nc.sync.dma_start(w_raw[1][:], w_rows[:, :, halves[1]])
         d_codes = tile("d_codes", [P, S], U32)
         d_codes_dealt = tile("d_codes_dealt", [P, S], U32)
         nc.vector.tensor_copy(d_codes[:], d_word_table[:].indirect(k1_t[:]))
@@ -112,8 +114,11 @@ def tile_picked_pqlayedblift_none_p_kernel(tc, x_words, x_scales, d_words, d_sca
                     acc = product(bank(f"h_first{a}", [P, W])[:], d_codes_dealt, d_plane, t, x_codes, x_plane, cols)
                     nc.vector.tensor_scalar(h_t[:, cols], acc, 0.0625, None, ALU.mult)
             else:
-                acc = product(bank(f"h_acc{t}", [P, S], tag=f"h_first{t % 2}")[:], d_codes_dealt, d_plane, t, x_codes, x_plane, whole)
-                nc.scalar.activation(h_t[:], acc, ACT.Copy, scale=0.0625)
+                acc = product(bank(f"h_acc{t}", [P, S], tag=f"h_first{(t + 1) % 2}")[:], d_codes_dealt, d_plane, t, x_codes, x_plane, whole)
+                if t == 1:
+                    nc.vector.tensor_scalar(h_t[:], acc, 0.0625, None, ALU.mult)
+                else:
+                    nc.scalar.activation(h_t[:], acc, ACT.Copy, scale=0.0625)
             h.append(h_t)
             sg_t = tile(f"sg{t}", [P, S], F32)
             for cols in halves:
@@ -130,22 +135,16 @@ def tile_picked_pqlayedblift_none_p_kernel(tc, x_words, x_scales, d_words, d_sca
         def interleave(copy, grouped, planes):
             copy(grouped.rearrange("p (c i) t -> p c t i", i=4), planes.rearrange("p t (c i) -> p c t i", i=4))
 
-        def quantize_w(a, tag):
-            w_grouped = tile(f"w_grouped{a}", [P, W, PACK], BF16, tag=tag)
-            interleave(nc.vector.tensor_copy, w_grouped[:], w_raw[:, :, halves[a]])
-            quantize(w_codes, w_plane, halves[a], w_grouped[:])
-
-        quantize_w(0, "sg_copy0")
-
         z_planes = tile("z_planes", [P, PACK, S], BF16)
-        diff = [tile(f"diff{t}", [P, S], F32) for t in range(PACK)]
+        diff = [tile(f"diff{t}", [P, S], F32, tag=f"diff{t % 2}") for t in range(PACK)]
 
-        def fetch_on_vector(t, parts):
-            span = slice(parts[0].start, parts[-1].stop)
-            sg_copy = tile(f"sg_copy{t}", [P, S], F32)
-            nc.vector.tensor_copy(sg_copy[:, span], sg[t][:, span])
-            for cols in parts:
-                nc.vector.tensor_tensor(diff[t][:, cols], sg[t][:].indirect(n2_t[:, entries(cols)]), sg_copy[:, cols], ALU.subtract)
+        def copy_sg(t, cols):
+            sg_copy = tile(f"sg_copy{t}", [P, S], F32, tag="x_byte_table")
+            nc.vector.tensor_copy(sg_copy[:, cols], sg[t][:, cols])
+            return sg_copy
+
+        def fetch_on_vector(t, cols, sg_copy):
+            nc.vector.tensor_tensor(diff[t][:, cols], sg[t][:].indirect(n2_t[:, entries(cols)]), sg_copy[:, cols], ALU.subtract)
 
         def fetch_on_scalar(t, cols):
             fetched = tile(f"fetched{t}_{cols.start}", [P, W], F32)
@@ -155,13 +154,20 @@ def tile_picked_pqlayedblift_none_p_kernel(tc, x_words, x_scales, d_words, d_sca
         def make_z(t, cols):
             nc.vector.scalar_tensor_tensor(z_planes[:, t, cols], diff[t][:, cols], gain_t[:, t : t + 1], h[t][:, cols], ALU.mult, ALU.mult)
 
-        for t in range(2):
-            fetch_on_vector(t, halves)
-            make_z(t, whole)
+        w_grouped = tile("w_grouped0", [P, W, PACK], BF16)
+        interleave(nc.vector.tensor_copy, w_grouped[:], w_raw[0][:])
+        sg_copy = copy_sg(0, whole)
+        quantize(w_codes, w_plane, halves[0], w_grouped[:])
+        for t, ahead in ((0, whole), (1, halves[0])):
+            for cols in halves:
+                fetch_on_vector(t, cols, sg_copy)
+            make_z(t, halves[0])
+            sg_copy = copy_sg(t + 1, ahead)
+            make_z(t, halves[1])
+        fetch_on_vector(2, halves[0], sg_copy)
+        fetch_on_scalar(2, halves[1])
         for cols in halves:
-            fetch_on_scalar(2, cols)
-        make_z(2, whole)
-        for cols in halves:
+            make_z(2, cols)
             fetch_on_scalar(3, cols)
         for cols in halves:
             make_z(3, cols)
@@ -169,13 +175,17 @@ def tile_picked_pqlayedblift_none_p_kernel(tc, x_words, x_scales, d_words, d_sca
         z_grouped = [tile(f"z_grouped{a}", [P, W, PACK], BF16) for a in range(2)]
         z_codes = tile("z_codes", [P, S], U32)
         z_plane = tile("z_plane", [P, S], U8)
-        interleave(nc.scalar.copy, z_grouped[0][:], z_planes[:, :, halves[0]])
-        interleave(nc.vector.tensor_copy, z_grouped[1][:], z_planes[:, :, halves[1]])
-        for a in (1, 0):
+        for a, share in enumerate((160, 64)):
+            planes = z_planes[:, :, halves[a]]
+            interleave(nc.scalar.copy, z_grouped[a][:, :share, :], planes[:, :, :share])
+            interleave(nc.vector.tensor_copy, z_grouped[a][:, share:, :], planes[:, :, share:])
+        for a in range(2):
             quantize(z_codes, z_plane, halves[a], z_grouped[a][:])
-        quantize_w(1, "z_grouped0")
+        w_grouped = tile("w_grouped1", [P, W, PACK], BF16, tag="z_grouped1")
+        interleave(nc.vector.tensor_copy, w_grouped[:], w_raw[1][:])
+        quantize(w_codes, w_plane, halves[1], w_grouped[:])
 
-        pieces = [(0, halves[1]), (1, halves[1]), (0, halves[0]), (1, halves[0]), (2, whole), (3, whole)]
+        pieces = [(0, halves[0]), (1, halves[0]), (0, halves[1]), (1, halves[1]), (2, whole), (3, whole)]
         h2_acc = [[] for u in range(PACK)]
         for n, (u, cols) in enumerate(pieces):
             h2_acc[u].append((cols, product(bank(f"h2_acc{n}", [P, cols.stop - cols.start], tag=f"h_first{n - 4}" if n >= 4 else None)[:], w_codes, w_plane, u, z_codes, z_plane, cols)))
@@ -183,11 +193,13 @@ def tile_picked_pqlayedblift_none_p_kernel(tc, x_words, x_scales, d_words, d_sca
         pa = [tile(f"pa{u}", [P, W], F32) for u in range(PACK)]
         ra = [tile(f"ra{u}", [P, W], F32) for u in range(PACK)]
         rise = [tile(f"rise{u}", [P, W], F32) for u in range(PACK)]
-        res = [tile(f"res{u}", [P, S], F32, tag="h2_3" if u == 1 else None) for u in range(PACK)]
+        res = [tile(f"res{u}", [P, S], F32) for u in range(PACK)]
 
-        def pair(u):
-            nc.vector.tensor_tensor(ra[u][:], h2[u][:].indirect(n4_t[:]), pa[u][:], ALU.subtract)
-            nc.vector.scalar_tensor_tensor(rise[u][:], pa[u][:], -0.5, ra[u][:], ALU.mult, ALU.max)
+        def pair(blocks):
+            for u in blocks:
+                nc.vector.tensor_tensor(ra[u][:], h2[u][:].indirect(n4_t[:]), pa[u][:], ALU.subtract)
+            for u in blocks:
+                nc.vector.scalar_tensor_tensor(rise[u][:], pa[u][:], -0.5, ra[u][:], ALU.mult, ALU.max)
 
         def put_rb(u):
             nc.vector.tensor_tensor(res[u][:].indirect(n4_t[:]), rise[u][:], pa[u][:], ALU.add)
@@ -205,16 +217,17 @@ def tile_picked_pqlayedblift_none_p_kernel(tc, x_words, x_scales, d_words, d_sca
             for cols, acc in h2_acc[u]:
                 nc.scalar.copy(h2[u][:, cols], acc)
             nc.scalar.activation(pa[u][:], h2[u][:].indirect(n3_t[:]), ACT.Copy)
-        pair(0)
-        put_rb(0)
+        pair((0, 1))
+        kept, handed = slice(0, 160), slice(160, W)
+        nc.vector.tensor_tensor(res[0][:].indirect(n4_t[:, entries(kept)]), rise[0][:, kept], pa[0][:, kept], ALU.add)
+        pair((2, 3))
         for u in range(1, PACK):
-            pair(u)
-        put_ra(0)
-        store(0, nc.sync)
-        put_rb(1)
-        for u in range(2, PACK):
             put_ra(u)
+            if u == 2:
+                rb = tile("rb", [P, W - 160], F32, tag="ra2")
+                nc.vector.tensor_tensor(rb[:], rise[0][:, handed], pa[0][:, handed], ALU.add)
             put_rb(u)
             store(u, nc.sync)
-        put_ra(1)
-        store(1, nc.scalar)
+        nc.scalar.activation(res[0][:].indirect(n4_t[:, entries(handed)]), rb[:], ACT.Copy)
+        put_ra(0)
+        store(0, nc.scalar)

from contextlib import ExitStack

import concourse.mybir as mybir

F32 = mybir.dt.float32
BF16 = mybir.dt.bfloat16
I32 = mybir.dt.int32
U32 = mybir.dt.uint32
U16 = mybir.dt.uint16
U8 = mybir.dt.uint8
FP8X4 = mybir.dt.float8_e4m3fn_x4
ALU = mybir.AluOpType
ACT = mybir.ActivationFunctionType

P = 128
PACK = 4
T = 2048
S = 512
W = 256
FLOPS = 2 * 2 * 512 * 512 * 512


def tile_picked_pqlayedblift_none_p_kernel(tc, x_words, x_scales, d_words, d_scales, sl, th, gn, w1, offs, k1, n1, n2, n3, n4, out):
    nc = tc.nc
    with ExitStack() as ctx:
        sb = ctx.enter_context(tc.tile_pool(name="sb", bufs=1))
        ps = ctx.enter_context(tc.psum_pool(name="ps", bufs=1))

        def tile(name, shape, dtype, tag=None):
            return sb.tile(shape, dtype, name=name, tag=tag or name, align_bytes=64)

        def load_list(name, src):
            t = tile(name, list(src.shape), U16)
            nc.sync.dma_start(t[:], src)
            return t

        def load_rows(name, src):
            t = tile(name, [P, PACK], F32)
            nc.sync.dma_start(t[:], src.rearrange("(p t) o -> p (t o)", t=PACK))
            return t

        def clock(name, ap, dtype):
            c = tile(name, [P, 1], dtype)
            nc.gpsimd.tensor_copy(c[:], ap)

        halves = [slice(W * a, W * (a + 1)) for a in range(2)]
        whole = slice(0, S)

        def entries(cols):
            return slice(cols.start // 16, cols.stop // 16)

        d_byte_table = tile("d_byte_table", [P, T], U8)
        x_byte_table = tile("x_byte_table", [P, T], U8)
        nc.vector.memset(d_byte_table[:].bitcast(I32), 0)
        nc.gpsimd.memset(x_byte_table[:].bitcast(I32), 0)

        k1_t = load_list("k1_t", k1)
        offs_t = load_list("offs_t", offs)
        nc.sync.dma_start(d_byte_table[0:P:8, :].bitcast(I32), d_scales[0].bitcast(I32))
        for q in range(4):
            nc.sync.dma_start(x_byte_table[32 * q : 32 * q + 4, :].bitcast(I32), x_scales[0, 4 * q : 4 * q + 4, :].bitcast(I32))
        d_word_table = tile("d_word_table", [P, T], U32)
        nc.sync.dma_start(d_word_table[:].bitcast(I32), d_words[0].rearrange("p n t -> p (n t)").bitcast(I32))
        n1_t = load_list("n1_t", n1)
        sl_t = load_rows("sl_t", sl)
        th_t = load_rows("th_t", th)
        x_word_table = tile("x_word_table", [P, T], U32)
        nc.sync.dma_start(x_word_table[:].bitcast(I32), x_words[0].rearrange("p n t -> p (n t)").bitcast(I32))

        d_bytes = tile("d_bytes", [P, S], U8)
        nc.vector.tensor_copy(d_bytes[:], d_byte_table[:].indirect(k1_t[:]))
        d_bytes_dealt = tile("d_bytes_dealt", [P, S], U8)
        nc.vector.tensor_copy(d_bytes_dealt[:].rearrange("p (t b i) -> p b t i", t=PACK, i=16), d_bytes[:].rearrange("p (b i t) -> p b t i", t=PACK, i=16))
        d_plane = tile("d_plane", [P, S], U8)
        nc.vector.tensor_copy(d_plane[:].bitcast(I32), d_bytes_dealt[:].bitcast(I32))
        for r in range(1, 4):
            nc.scalar.dma_start(d_plane[r:P:32, :].bitcast(I32), d_bytes_dealt[8 * r : P : 32, :].bitcast(I32))
        x_plane = tile("x_plane", [P, S], U8)
        nc.vector.tensor_copy(x_plane[:], x_byte_table[:].indirect(offs_t[:]))
        w_rows = w1.rearrange("(p t) m -> p t m", t=PACK)
        w_raw = [tile("w_raw0", [P, PACK, W], F32, tag="x_byte_table"), tile("w_raw1", [P, PACK, W], F32)]
        nc.sync.dma_start(w_raw[0][:], w_rows[:, :, halves[0]])
        n2_t = load_list("n2_t", n2)
        gn_t = load_rows("gn_t", gn)
        n3_t = load_list("n3_t", n3)
        n4_t = load_list("n4_t", n4)
        nc.sync.dma_start(w_raw[1][:], w_rows[:, :, halves[1]])
        d_codes = tile("d_codes", [P, S], U32)
        d_codes_dealt = tile("d_codes_dealt", [P, S], U32)
        nc.vector.tensor_copy(d_codes[:], d_word_table[:].indirect(k1_t[:]))
        nc.vector.tensor_copy(d_codes_dealt[:].rearrange("p (t b i) -> p b t i", t=PACK, i=4), d_codes[:].rearrange("p (b i t) -> p b t i", t=PACK, i=4))
        x_codes = tile("x_codes", [P, S], U32)
        for cols in halves:
            nc.vector.tensor_copy(x_codes[:, cols], x_word_table[:].indirect(offs_t[:, entries(cols)]))
        bias_t = tile("bias_t", [P, PACK], F32)
        nc.vector.scalar_tensor_tensor(bias_t[:], sl_t[:], -1.0, th_t[:], ALU.mult, ALU.mult)
        gain_t = tile("gain_t", [P, PACK], F32)
        nc.vector.tensor_scalar(gain_t[:], gn_t[:], -1.5, None, ALU.mult)

        def bank(name, shape, tag=None):
            return ps.tile(shape, F32, name=name, tag=tag or name)

        def product(acc, codes_l, plane_l, block, codes_r, plane_r, cols):
            rows = slice(P * block, P * (block + 1))
            nc.tensor.matmul_mx(out=acc, lhsT=codes_l[:, rows].bitcast(FP8X4), lhsT_scale=plane_l[:, rows],
                                rhs=codes_r[:, cols].bitcast(FP8X4), rhs_scale=plane_r[:, cols], start=True, stop=True)
            return acc

        h, sg = [], []
        for t in range(PACK):
            h_t = tile(f"h{t}", [P, S], F32)
            if t == 0:
                for a, cols in enumerate(halves):
                    acc = product(bank(f"h_first{a}", [P, W])[:], d_codes_dealt, d_plane, t, x_codes, x_plane, cols)
                    nc.vector.tensor_scalar(h_t[:, cols], acc, 0.0625, None, ALU.mult)
            else:
                acc = product(bank(f"h_acc{t}", [P, S], tag=f"h_first{(t + 1) % 2}")[:], d_codes_dealt, d_plane, t, x_codes, x_plane, whole)
                if t == 1:
                    nc.vector.tensor_scalar(h_t[:], acc, 0.0625, None, ALU.mult)
                else:
                    nc.scalar.activation(h_t[:], acc, ACT.Copy, scale=0.0625)
            h.append(h_t)
            sg_t = tile(f"sg{t}", [P, S], F32)
            for cols in halves:
                nc.scalar.activation(sg_t[:, cols], h_t[:].indirect(n1_t[:, entries(cols)]), ACT.Sigmoid,
                                     bias=bias_t[:, t : t + 1], scale=sl_t[:, t : t + 1])
            sg.append(sg_t)

        w_codes = tile("w_codes", [P, S], U32)
        w_plane = tile("w_plane", [P, S], U8)

        def quantize(codes, plane, cols, grouped):
            nc.vector.quantize_mx(out=codes[:, cols].bitcast(FP8X4), scales=plane[:, cols], in_=grouped.rearrange("p c t -> p (c t)"))

        def interleave(copy, grouped, planes):
            copy(grouped.rearrange("p (c i) t -> p c t i", i=4), planes.rearrange("p t (c i) -> p c t i", i=4))

        z_planes = tile("z_planes", [P, PACK, S], BF16)
        diff = [tile(f"diff{t}", [P, S], F32, tag=f"diff{t % 2}") for t in range(PACK)]

        def copy_sg(t, cols):
            sg_copy = tile(f"sg_copy{t}", [P, S], F32, tag="x_byte_table")
            nc.vector.tensor_copy(sg_copy[:, cols], sg[t][:, cols])
            return sg_copy

        def fetch_on_vector(t, cols, sg_copy):
            nc.vector.tensor_tensor(diff[t][:, cols], sg[t][:].indirect(n2_t[:, entries(cols)]), sg_copy[:, cols], ALU.subtract)

        def fetch_on_scalar(t, cols):
            fetched = tile(f"fetched{t}_{cols.start}", [P, W], F32)
            nc.scalar.activation(fetched[:], sg[t][:].indirect(n2_t[:, entries(cols)]), ACT.Copy)
            nc.vector.tensor_tensor(diff[t][:, cols], fetched[:], sg[t][:, cols], ALU.subtract)

        def make_z(t, cols):
            nc.vector.scalar_tensor_tensor(z_planes[:, t, cols], diff[t][:, cols], gain_t[:, t : t + 1], h[t][:, cols], ALU.mult, ALU.mult)

        w_grouped = tile("w_grouped0", [P, W, PACK], BF16)
        interleave(nc.vector.tensor_copy, w_grouped[:], w_raw[0][:])
        sg_copy = copy_sg(0, whole)
        quantize(w_codes, w_plane, halves[0], w_grouped[:])
        for t, ahead in ((0, whole), (1, halves[0])):
            for cols in halves:
                fetch_on_vector(t, cols, sg_copy)
            make_z(t, halves[0])
            sg_copy = copy_sg(t + 1, ahead)
            make_z(t, halves[1])
        fetch_on_vector(2, halves[0], sg_copy)
        fetch_on_scalar(2, halves[1])
        for cols in halves:
            make_z(2, cols)
            fetch_on_scalar(3, cols)
        for cols in halves:
            make_z(3, cols)

        z_grouped = [tile(f"z_grouped{a}", [P, W, PACK], BF16) for a in range(2)]
        z_codes = tile("z_codes", [P, S], U32)
        z_plane = tile("z_plane", [P, S], U8)
        for a, share in enumerate((160, 64)):
            planes = z_planes[:, :, halves[a]]
            interleave(nc.scalar.copy, z_grouped[a][:, :share, :], planes[:, :, :share])
            interleave(nc.vector.tensor_copy, z_grouped[a][:, share:, :], planes[:, :, share:])
        for a in range(2):
            quantize(z_codes, z_plane, halves[a], z_grouped[a][:])
        w_grouped = tile("w_grouped1", [P, W, PACK], BF16, tag="z_grouped1")
        interleave(nc.vector.tensor_copy, w_grouped[:], w_raw[1][:])
        quantize(w_codes, w_plane, halves[1], w_grouped[:])

        pieces = [(0, halves[0]), (1, halves[0]), (0, halves[1]), (1, halves[1]), (2, whole), (3, whole)]
        h2_acc = [[] for u in range(PACK)]
        for n, (u, cols) in enumerate(pieces):
            h2_acc[u].append((cols, product(bank(f"h2_acc{n}", [P, cols.stop - cols.start], tag=f"h_first{n - 4}" if n >= 4 else None)[:], w_codes, w_plane, u, z_codes, z_plane, cols)))
        h2 = [tile(f"h2_{u}", [P, S], F32) for u in range(PACK)]
        pa = [tile(f"pa{u}", [P, W], F32) for u in range(PACK)]
        ra = [tile(f"ra{u}", [P, W], F32) for u in range(PACK)]
        rise = [tile(f"rise{u}", [P, W], F32) for u in range(PACK)]
        res = [tile(f"res{u}", [P, S], F32) for u in range(PACK)]

        def pair(blocks):
            for u in blocks:
                nc.vector.tensor_tensor(ra[u][:], h2[u][:].indirect(n4_t[:]), pa[u][:], ALU.subtract)
            for u in blocks:
                nc.vector.scalar_tensor_tensor(rise[u][:], pa[u][:], -0.5, ra[u][:], ALU.mult, ALU.max)

        def put_rb(u):
            nc.vector.tensor_tensor(res[u][:].indirect(n4_t[:]), rise[u][:], pa[u][:], ALU.add)

        def put_ra(u):
            nc.scalar.activation(res[u][:].indirect(n3_t[:]), ra[u][:], ACT.Copy)

        def store(u, eng):
            eng.dma_start(out[P * u : P * (u + 1), :], res[u][:])

        for cols, acc in h2_acc[0]:
            nc.scalar.copy(h2[0][:, cols], acc)
        nc.vector.tensor_copy(pa[0][:], h2[0][:].indirect(n3_t[:]))
        for u in range(1, PACK):
            for cols, acc in h2_acc[u]:
                nc.scalar.copy(h2[u][:, cols], acc)
            nc.scalar.activation(pa[u][:], h2[u][:].indirect(n3_t[:]), ACT.Copy)
        pair((0, 1))
        kept, handed = slice(0, 160), slice(160, W)
        nc.vector.tensor_tensor(res[0][:].indirect(n4_t[:, entries(kept)]), rise[0][:, kept], pa[0][:, kept], ALU.add)
        pair((2, 3))
        for u in range(1, PACK):
            put_ra(u)
            if u == 2:
                rb = tile("rb", [P, W - 160], F32, tag="ra2")
                nc.vector.tensor_tensor(rb[:], rise[0][:, handed], pa[0][:, handed], ALU.add)
            put_rb(u)
            store(u, nc.sync)
        nc.scalar.activation(res[0][:].indirect(n4_t[:, entries(handed)]), rb[:], ACT.Copy)
        put_ra(0)
        store(0, nc.scalar)
